import numpy as np
import ml_dtypes


def mxq(x, axis, fmt="e4m3"):
    dtype, down = {"e4m3": (ml_dtypes.float8_e4m3fn, 7), "e5m2": (ml_dtypes.float8_e5m2, 14)}[fmt]
    v = np.moveaxis(np.asarray(x, np.float32).astype(ml_dtypes.bfloat16).astype(np.float64), axis, -1)
    blocks = v.reshape(v.shape[:-1] + (-1, 32))
    amax = np.abs(blocks).max(-1, keepdims=True)
    byte = np.maximum(np.where(amax > 0, np.frexp(amax)[1] - 1 + 127, 0) - down, 1)
    scale = np.exp2(byte - 127.0)
    codes = (blocks / scale).astype(np.float32).astype(dtype).astype(np.float64)
    return np.moveaxis((codes * scale).reshape(v.shape), -1, axis)


WIDE = False


def mx_kscale(k):
    if not WIDE:
        return np.ones(k)
    levels = np.array([10, -10, 5, -5, 0])
    if k % 512:
        return np.exp2(np.random.permutation(np.resize(levels, k // 32))).repeat(32)
    a = np.empty((k // 512, 16))
    for p in range(k // 512):
        a[p, :8] = np.random.permutation(np.resize(levels, 8))
        for g in range(8):
            far = levels[np.abs(levels - a[p, g]) >= 10]
            a[p, g + 8] = far[np.random.randint(len(far))]
    return np.exp2(a.ravel()).repeat(32)


def f64(x):
    return np.asarray(x).astype(np.float64)


def striped(idx):
    return np.tile(idx.reshape(-1, 16).T, (8, 1)).astype(np.uint16)


def unstriped(offs):
    return offs[:16].T.reshape(-1).astype(np.int64)


def striped8(idx):
    return np.concatenate([x.reshape(-1, 16).T for x in idx]).astype(np.uint16)


def runs(offs, k):
    lists = np.stack([offs[16 * r : 16 * r + 16].T.reshape(-1) for r in range(8)]).astype(np.int64)
    return lists[np.arange(k) % 512 // 64]


def pack_weight(w):
    k, n = w.shape
    w = f64(np.asarray(w, np.float32).astype(ml_dtypes.bfloat16)).reshape(k // 32, 32, n)
    amax = np.abs(w).max(1)
    byte = np.clip(np.where(amax > 0, np.frexp(amax)[1] - 1 + 127 - 7, 1), 1, 254)
    scaled = (w * np.exp2(127.0 - byte)[:, None, :]).reshape(k, n).astype(np.float32)
    words = np.ascontiguousarray(scaled.reshape(k // 512, 128, 4, n).transpose(0, 1, 3, 2)).astype(ml_dtypes.float8_e4m3fn).view(np.uint8)
    return words, np.ascontiguousarray(byte.astype(np.uint8).reshape(k // 512, 16, n))


def unpack_weight(words, scales):
    g, p, n, _ = words.shape
    vals = np.ascontiguousarray(words).view(ml_dtypes.float8_e4m3fn).astype(np.float64) * np.repeat(np.exp2(scales.astype(np.float64) - 127.0), 8, axis=1)[..., None]
    return vals.transpose(0, 1, 3, 2).reshape(g * 512, n)


def relu(v):
    return np.maximum(v, 0.0)


K, T, S, N, H, U = 512, 2048, 256, 512, 512, 1024


def setup_inputs():
    n = np.random.standard_normal
    s = mx_kscale(K)[:, None]
    u = mx_kscale(H)
    packed_xT = pack_weight(n((K, T)) * s)
    return {
        "x_words": packed_xT[0],
        "x_scales": packed_xT[1],
        "w1": (n((K, H)) / np.sqrt(2 * K) / s).astype(np.float32),
        "w2": (n((K, H)) / np.sqrt(2 * K) / s).astype(np.float32),
        "gn": (np.random.uniform(0.5, 1.5, (H, 1)) * u[:, None]).astype(np.float32),
        "w3": (n((H, N)) / np.sqrt(H) / u[:, None]).astype(np.float32),
        "offs": striped8(np.random.randint(0, T, (8, S))),
        "hz": striped8(np.random.randint(0, T, (8, S))),
        "n1": striped(np.random.permutation(S)),
        "n2": striped(np.random.permutation(U)[:S]),
        "n3": striped(np.random.permutation(S)),
    }


def reference(x_words, x_scales, w1, w2, gn, w3, offs, hz, n1, n2, n3):
    xq = unpack_weight(x_words, x_scales)[np.arange(K)[:, None], runs(offs, K)]
    x_hz = unpack_weight(x_words, x_scales)[np.arange(K)[:, None], runs(hz, K)]
    y = mxq(f64(w1), 0, "e4m3").T @ xq + mxq(f64(w2), 0, "e4m3").T @ x_hz
    ds = np.zeros((H, S))
    ds[:, unstriped(n1)] = y
    z = f64(gn) * (y - ds)
    h = mxq(f64(w3), 0, "e4m3").T @ mxq(z, 0, "e4m3")
    nw = h - (relu(h[:, unstriped(n3)]))
    out = np.zeros((N, U))
    out[:, unstriped(n2)] = nw
    return out

@@ -1,0 +1,154 @@
+from contextlib import ExitStack
+
+import concourse.mybir as mybir
+
+K, T, S, N, H, U = 512, 2048, 256, 512, 512, 1024
+FLOPS = 2 * (2 * K * H * S + H * N * S)
+
+F32 = mybir.dt.float32
+BF16 = mybir.dt.bfloat16
+I32 = mybir.dt.int32
+U32 = mybir.dt.uint32
+U16 = mybir.dt.uint16
+U8 = mybir.dt.uint8
+FP8X4 = mybir.dt.float8_e4m3fn_x4
+ALU = mybir.AluOpType
+COPY = mybir.ActivationFunctionType.Copy
+
+P = 128
+PACK = 4
+SEND_WINDOW = 2 * S
+FETCH_WINDOW = S + 16
+
+
+def tile_picked_dhlsendmxpagez_none_p_kernel(tc, x_words, x_scales, w1, w2, gn, w3, offs, hz, n1, n2, n3, out):
+    nc = tc.nc
+    with ExitStack() as ctx:
+        keep = ctx.enter_context(tc.tile_pool(name="keep", bufs=1))
+        psum = ctx.enter_context(tc.psum_pool(name="psum", bufs=1))
+
+        lists = {}
+        for name in ("offs", "hz", "n1", "n3", "n2"):
+            lists[name] = keep.tile([P, S // 16], U16, name="list_" + name)
+        nc.sync.dma_start(lists["offs"][:], offs)
+        nc.sync.dma_start(lists["hz"][:], hz)
+
+        scale_table = keep.tile([P, T], U8, name="scale_table")
+        nc.vector.memset(scale_table[:].bitcast(I32), 0)
+        for i in range(2):
+            nc.scalar.dma_start(scale_table[i:P:16, :].bitcast(I32), x_scales[0, i:16:2, :].bitcast(I32))
+
+        raw = {}
+        for name, w in (("w1", w1), ("w2", w2)):
+            raw[name] = keep.tile([P, PACK, H], F32, name="raw_" + name, tag="raw_" + name)
+            nc.sync.dma_start(raw[name][:], w.rearrange("(p j) c -> p j c", j=PACK))
+        word_table = keep.tile([P, T], U32, name="word_table")
+        nc.sync.dma_start(word_table[:].bitcast(I32), x_words[0].rearrange("p c r -> p (c r)").bitcast(I32))
+        nc.sync.dma_start(lists["n1"][:], n1)
+        gain = keep.tile([P, PACK], F32, name="gain")
+        nc.gpsimd.dma_start(gain[:], gn.rearrange("(p t) o -> p (t o)", t=PACK))
+        nc.sync.dma_start(lists["n3"][:], n3)
+        nc.sync.dma_start(lists["n2"][:], n2)
+
+        pages = []
+        relus = []
+        for m in range(N // P):
+            page = keep.tile([P, U], F32, name="page%d" % m)
+            if m < 2:
+                nc.vector.memset(page[:].bitcast(I32), 0)
+            else:
+                nc.scalar.activation(page[:], pages[m - 2][:], COPY)
+            pages.append(page)
+            relu_h = keep.tile([P, FETCH_WINDOW], F32, name="relu%d" % m)
+            relus.append(relu_h)
+
+        picked_scales = keep.tile([P, 2 * S], U8, name="picked_scales")
+        for u, name in enumerate(("offs", "hz")):
+            nc.vector.tensor_copy(picked_scales[:, u * S : (u + 1) * S], scale_table[:].indirect(lists[name][:]))
+        x_plane = keep.tile([P, 2 * S], U8, name="x_plane", align_bytes=64)
+        nc.vector.tensor_copy(x_plane[:].bitcast(I32), picked_scales[:].bitcast(I32))
+        for i in range(2):
+            nc.scalar.dma_start(x_plane[2 + i : P : 32, :].bitcast(I32), picked_scales[16 + i : P : 32, :].bitcast(I32))
+
+        codes = {}
+        planes = {}
+
+        def quantize(name, grouped, width):
+            codes[name] = keep.tile([P, width], U32, name="codes_" + name, align_bytes=64)
+            planes[name] = keep.tile([P, width], U8, name="plane_" + name, align_bytes=64)
+            nc.vector.quantize_mx(out=codes[name][:].bitcast(FP8X4), scales=planes[name][:], in_=grouped[:])
+
+        for name in ("w1", "w2"):
+            for half in range(2):
+                grouped = keep.tile([P, 2 * PACK * P], BF16, name="grouped_%s_%d" % (name, half), align_bytes=64)
+                dealt = grouped[:].rearrange("p (t m j) -> p m j t", t=2, j=PACK)
+                source = raw[name][:].rearrange("p j (m t) -> p m j t", t=PACK)[:, :, :, 2 * half : 2 * half + 2]
+                if half == 0:
+                    nc.vector.tensor_copy(dealt, source)
+                else:
+                    nc.scalar.activation(dealt, source, COPY)
+                quantize("%s_%d" % (name, half), grouped, 2 * P)
+
+        raw["w3"] = keep.tile([P, PACK, N], F32, name="raw_w3", tag="raw_w1")
+        nc.sync.dma_start(raw["w3"][:], w3.rearrange("(p j) c -> p j c", j=PACK))
+
+        picked = []
+        for name in ("offs", "hz"):
+            words = keep.tile([P, S], U32, name="picked_" + name, align_bytes=64)
+            nc.vector.tensor_copy(words[:], word_table[:].indirect(lists[name][:]))
+            picked.append(words)
+
+        z = keep.tile([P, S * PACK], BF16, name="z", align_bytes=64)
+        gained = []
+        sent = []
+        for t in range(PACK):
+            cols = slice(t % 2 * P, (t % 2 + 1) * P)
+            y_bank = psum.tile([P, S], F32, name="y%d" % t)
+            for u, name in enumerate(("w1_%d" % (t // 2), "w2_%d" % (t // 2))):
+                nc.tensor.matmul_mx(
+                    out=y_bank[:],
+                    lhsT=codes[name][:, cols].bitcast(FP8X4),
+                    lhsT_scale=planes[name][:, cols],
+                    rhs=picked[u][:].bitcast(FP8X4),
+                    rhs_scale=x_plane[:, u * S : (u + 1) * S],
+                    start=(u == 0),
+                    stop=(u == 1),
+                )
+            gy = keep.tile([P, S], F32, name="gy%d" % t)
+            nc.vector.tensor_scalar(gy[:], y_bank[:], gain[:, t : t + 1], None, ALU.mult)
+            gained.append(gy)
+            ds = keep.tile([P, SEND_WINDOW], F32, name="ds%d" % t)
+            nc.scalar.activation(ds[:].indirect(lists["n1"][:]), gy[:], COPY)
+            sent.append(ds)
+
+        grouped = keep.tile([P, PACK * N], BF16, name="grouped_w3", align_bytes=64)
+        nc.vector.tensor_copy(
+            grouped[:].rearrange("p (c i j) -> p c j i", i=4, j=PACK),
+            raw["w3"][:].rearrange("p j (c i) -> p c j i", i=4),
+        )
+        quantize("w3", grouped, N)
+
+        z_slots = z[:].rearrange("p (c t) -> p t c", t=PACK)
+        for t in range(PACK):
+            nc.vector.tensor_tensor(z_slots[:, t, :], gained[t][:], sent[t][:, 0:S], ALU.subtract)
+        quantize("z", z, S)
+
+        for m in range(N // P):
+            cols = slice(m * P, (m + 1) * P)
+            h_bank = psum.tile([P, S], F32, name="h%d" % m)
+            nc.tensor.matmul_mx(
+                out=h_bank[:],
+                lhsT=codes["w3"][:, cols].bitcast(FP8X4),
+                lhsT_scale=planes["w3"][:, cols],
+                rhs=codes["z"][:].bitcast(FP8X4),
+                rhs_scale=planes["z"][:],
+                start=True,
+                stop=True,
+            )
+            nc.vector.tensor_scalar(relus[m][:, 0:S], h_bank[:], 0.0, None, ALU.max)
+            fetched = keep.tile([P, S], F32, name="fetched%d" % m)
+            nc.scalar.activation(fetched[:], relus[m][:].indirect(lists["n3"][:]), COPY)
+            nw = keep.tile([P, S], F32, name="nw%d" % m)
+            nc.vector.tensor_tensor(nw[:], h_bank[:], fetched[:], ALU.subtract)
+            nc.scalar.activation(pages[m][:].indirect(lists["n2"][:]), nw[:], COPY)
+            nc.sync.dma_start(out[cols, :], pages[m][:])

@@ -30,25 +30,24 @@ def tile_picked_dhlsendmxpagez_none_p_kernel(tc, x_words, x_scales, w1, w2, gn, 
         lists = {}
         for name in ("offs", "hz", "n1", "n3", "n2"):
             lists[name] = keep.tile([P, S // 16], U16, name="list_" + name)
+        raw = {}
+        w1_rows = w1.rearrange("(p j) c -> p j c", j=PACK)
+        raw["w1"] = keep.tile([P, PACK, H], F32, name="raw_w1")
+        nc.sync.dma_start(raw["w1"][:, 0:2, :], w1_rows[:, 0:2, :])
         nc.sync.dma_start(lists["offs"][:], offs)
         nc.sync.dma_start(lists["hz"][:], hz)
 
         scale_table = keep.tile([P, T], U8, name="scale_table")
         nc.vector.memset(scale_table[:].bitcast(I32), 0)
         for i in range(2):
-            nc.scalar.dma_start(scale_table[i:P:16, :].bitcast(I32), x_scales[0, i:16:2, :].bitcast(I32))
+            nc.sync.dma_start(scale_table[i:P:16, :].bitcast(I32), x_scales[0, i:16:2, :].bitcast(I32))
 
-        raw = {}
-        for name, w in (("w1", w1), ("w2", w2)):
-            raw[name] = keep.tile([P, PACK, H], F32, name="raw_" + name, tag="raw_" + name)
-            nc.sync.dma_start(raw[name][:], w.rearrange("(p j) c -> p j c", j=PACK))
+        nc.sync.dma_start(raw["w1"][:, 2:4, :], w1_rows[:, 2:4, :])
         word_table = keep.tile([P, T], U32, name="word_table")
         nc.sync.dma_start(word_table[:].bitcast(I32), x_words[0].rearrange("p c r -> p (c r)").bitcast(I32))
-        nc.sync.dma_start(lists["n1"][:], n1)
-        gain = keep.tile([P, PACK], F32, name="gain")
-        nc.gpsimd.dma_start(gain[:], gn.rearrange("(p t) o -> p (t o)", t=PACK))
-        nc.sync.dma_start(lists["n3"][:], n3)
-        nc.sync.dma_start(lists["n2"][:], n2)
+        w2_rows = w2.rearrange("(p j) c -> p j c", j=PACK)
+        w2_early = keep.tile([P, PACK - 1, H], F32, name="w2_early")
+        nc.sync.dma_start(w2_early[:], w2_rows[:, 0 : PACK - 1, :])
 
         pages = []
         relus = []
@@ -68,29 +67,44 @@ def tile_picked_dhlsendmxpagez_none_p_kernel(tc, x_words, x_scales, w1, w2, gn, 
         x_plane = keep.tile([P, 2 * S], U8, name="x_plane", align_bytes=64)
         nc.vector.tensor_copy(x_plane[:].bitcast(I32), picked_scales[:].bitcast(I32))
         for i in range(2):
-            nc.scalar.dma_start(x_plane[2 + i : P : 32, :].bitcast(I32), picked_scales[16 + i : P : 32, :].bitcast(I32))
+            nc.sync.dma_start(x_plane[2 + i : P : 32, :].bitcast(I32), picked_scales[16 + i : P : 32, :].bitcast(I32))
 
-        codes = {}
-        planes = {}
-
-        def quantize(name, grouped, width):
-            codes[name] = keep.tile([P, width], U32, name="codes_" + name, align_bytes=64)
-            planes[name] = keep.tile([P, width], U8, name="plane_" + name, align_bytes=64)
-            nc.vector.quantize_mx(out=codes[name][:].bitcast(FP8X4), scales=planes[name][:], in_=grouped[:])
-
-        for name in ("w1", "w2"):
-            for half in range(2):
-                grouped = keep.tile([P, 2 * PACK * P], BF16, name="grouped_%s_%d" % (name, half), align_bytes=64)
-                dealt = grouped[:].rearrange("p (t m j) -> p m j t", t=2, j=PACK)
-                source = raw[name][:].rearrange("p j (m t) -> p m j t", t=PACK)[:, :, :, 2 * half : 2 * half + 2]
-                if half == 0:
-                    nc.vector.tensor_copy(dealt, source)
-                else:
-                    nc.scalar.activation(dealt, source, COPY)
-                quantize("%s_%d" % (name, half), grouped, 2 * P)
-
-        raw["w3"] = keep.tile([P, PACK, N], F32, name="raw_w3", tag="raw_w1")
+        w2_last = keep.tile([P, H], F32, name="w2_last")
+        nc.sync.dma_start(w2_last[:], w2_rows[:, PACK - 1, :])
+        nc.sync.dma_start(lists["n1"][:], n1)
+        gain = keep.tile([P, PACK], F32, name="gain")
+        nc.sync.dma_start(gain[:], gn.rearrange("(p t) o -> p (t o)", t=PACK))
+        raw["w3"] = keep.tile([P, PACK, N], F32, name="raw_w3")
         nc.sync.dma_start(raw["w3"][:], w3.rearrange("(p j) c -> p j c", j=PACK))
+        nc.sync.dma_start(lists["n3"][:], n3)
+        nc.sync.dma_start(lists["n2"][:], n2)
+
+        def mx_tiles(name, width):
+            codes = keep.tile([P, width], U32, name="codes_" + name, align_bytes=64)
+            plane = keep.tile([P, width], U8, name="plane_" + name, align_bytes=64)
+            return codes, plane
+
+        def quantize(operand, grouped, first, width):
+            codes, plane = operand
+            nc.vector.quantize_mx(
+                out=codes[:, first : first + width].bitcast(FP8X4),
+                scales=plane[:, first : first + width],
+                in_=grouped[:, PACK * first : PACK * (first + width)],
+            )
+
+        def cast(half, dealt, source):
+            if half == 0:
+                nc.vector.tensor_copy(dealt, source)
+            else:
+                nc.scalar.activation(dealt, source, COPY)
+
+        w1_mx = []
+        for half in range(2):
+            grouped = keep.tile([P, 2 * PACK * P], BF16, name="grouped_w1_%d" % half, align_bytes=64)
+            dealt = grouped[:].rearrange("p (t m j) -> p m j t", t=2, j=PACK)
+            cast(half, dealt, raw["w1"][:].rearrange("p j (m t) -> p m j t", t=PACK)[:, :, :, 2 * half : 2 * half + 2])
+            w1_mx.append(mx_tiles("w1_%d" % half, 2 * P))
+            quantize(w1_mx[half], grouped, 0, 2 * P)
 
         picked = []
         for name in ("offs", "hz"):
@@ -98,17 +112,34 @@ def tile_picked_dhlsendmxpagez_none_p_kernel(tc, x_words, x_scales, w1, w2, gn, 
             nc.vector.tensor_copy(words[:], word_table[:].indirect(lists[name][:]))
             picked.append(words)
 
-        z = keep.tile([P, S * PACK], BF16, name="z", align_bytes=64)
+        w2_mx = []
+        w2_grouped = []
+        early = w2_early[:].rearrange("p j (m t) -> p m j t", t=PACK)
+        last = w2_last[:].rearrange("p (m t) -> p m t", t=PACK)
+        for half in range(2):
+            grouped = keep.tile([P, 2 * PACK * P], BF16, name="grouped_w2_%d" % half, align_bytes=64)
+            dealt = grouped[:].rearrange("p (t m j) -> p m j t", t=2, j=PACK)
+            cast(half, dealt[:, :, 0 : PACK - 1, :], early[:, :, :, 2 * half : 2 * half + 2])
+            w2_grouped.append(grouped)
+            w2_mx.append(mx_tiles("w2_%d" % half, 2 * P))
+        dealt = w2_grouped[0][:].rearrange("p (t m j) -> p m j t", t=2, j=PACK)
+        for t in range(2):
+            cast(0, dealt[:, :, PACK - 1, t], last[:, :, t])
+            quantize(w2_mx[0], w2_grouped[0], t * P, P)
+        dealt = w2_grouped[1][:].rearrange("p (t m j) -> p m j t", t=2, j=PACK)
+        cast(1, dealt[:, :, PACK - 1, :], last[:, :, 2:4])
+        quantize(w2_mx[1], w2_grouped[1], 0, 2 * P)
+
         gained = []
         sent = []
         for t in range(PACK):
             cols = slice(t % 2 * P, (t % 2 + 1) * P)
             y_bank = psum.tile([P, S], F32, name="y%d" % t)
-            for u, name in enumerate(("w1_%d" % (t // 2), "w2_%d" % (t // 2))):
+            for u, (codes, plane) in enumerate((w1_mx[t // 2], w2_mx[t // 2])):
                 nc.tensor.matmul_mx(
                     out=y_bank[:],
-                    lhsT=codes[name][:, cols].bitcast(FP8X4),
-                    lhsT_scale=planes[name][:, cols],
+                    lhsT=codes[:, cols].bitcast(FP8X4),
+                    lhsT_scale=plane[:, cols],
                     rhs=picked[u][:].bitcast(FP8X4),
                     rhs_scale=x_plane[:, u * S : (u + 1) * S],
                     start=(u == 0),
@@ -121,30 +152,38 @@ def tile_picked_dhlsendmxpagez_none_p_kernel(tc, x_words, x_scales, w1, w2, gn, 
             nc.scalar.activation(ds[:].indirect(lists["n1"][:]), gy[:], COPY)
             sent.append(ds)
 
-        grouped = keep.tile([P, PACK * N], BF16, name="grouped_w3", align_bytes=64)
+        grouped = keep.tile([P, PACK * N], BF16, name="grouped_w3", tag="grouped_w3", align_bytes=64)
         nc.vector.tensor_copy(
             grouped[:].rearrange("p (c i j) -> p c j i", i=4, j=PACK),
             raw["w3"][:].rearrange("p j (c i) -> p c j i", i=4),
         )
-        quantize("w3", grouped, N)
+        w3_mx = mx_tiles("w3", N)
+        quantize(w3_mx, grouped, 0, N)
 
+        z = keep.tile([P, S * PACK], BF16, name="z", tag="grouped_w3", align_bytes=64)
         z_slots = z[:].rearrange("p (c t) -> p t c", t=PACK)
-        for t in range(PACK):
+        for t in range(PACK - 1):
             nc.vector.tensor_tensor(z_slots[:, t, :], gained[t][:], sent[t][:, 0:S], ALU.subtract)
-        quantize("z", z, S)
+        halves = [slice(0, S // 2), slice(S // 2, S)]
+        for places in halves:
+            nc.vector.tensor_tensor(z_slots[:, PACK - 1, places], gained[-1][:, places], sent[-1][:, places], ALU.subtract)
+        z_mx = mx_tiles("z", S)
+        for places in halves:
+            quantize(z_mx, z, places.start, S // 2)
 
         for m in range(N // P):
             cols = slice(m * P, (m + 1) * P)
             h_bank = psum.tile([P, S], F32, name="h%d" % m)
-            nc.tensor.matmul_mx(
-                out=h_bank[:],
-                lhsT=codes["w3"][:, cols].bitcast(FP8X4),
-                lhsT_scale=planes["w3"][:, cols],
-                rhs=codes["z"][:].bitcast(FP8X4),
-                rhs_scale=planes["z"][:],
-                start=True,
-                stop=True,
-            )
+            for places in halves if m == 0 else [slice(0, S)]:
+                nc.tensor.matmul_mx(
+                    out=h_bank[:, places],
+                    lhsT=w3_mx[0][:, cols].bitcast(FP8X4),
+                    lhsT_scale=w3_mx[1][:, cols],
+                    rhs=z_mx[0][:, places].bitcast(FP8X4),
+                    rhs_scale=z_mx[1][:, places],
+                    start=True,
+                    stop=True,
+                )
             nc.vector.tensor_scalar(relus[m][:, 0:S], h_bank[:], 0.0, None, ALU.max)
             fetched = keep.tile([P, S], F32, name="fetched%d" % m)
             nc.scalar.activation(fetched[:], relus[m][:].indirect(lists["n3"][:]), COPY)

@@ -14,6 +14,7 @@ U8 = mybir.dt.uint8
 FP8X4 = mybir.dt.float8_e4m3fn_x4
 ALU = mybir.AluOpType
 COPY = mybir.ActivationFunctionType.Copy
+RELU = mybir.ActivationFunctionType.Relu
 
 P = 128
 PACK = 4
@@ -46,8 +47,8 @@ def tile_picked_dhlsendmxpagez_none_p_kernel(tc, x_words, x_scales, w1, w2, gn, 
         word_table = keep.tile([P, T], U32, name="word_table")
         nc.sync.dma_start(word_table[:].bitcast(I32), x_words[0].rearrange("p c r -> p (c r)").bitcast(I32))
         w2_rows = w2.rearrange("(p j) c -> p j c", j=PACK)
-        w2_early = keep.tile([P, PACK - 1, H], F32, name="w2_early")
-        nc.sync.dma_start(w2_early[:], w2_rows[:, 0 : PACK - 1, :])
+        raw["w2"] = keep.tile([P, PACK, H], F32, name="raw_w2")
+        nc.sync.dma_start(raw["w2"][:, 0 : PACK - 1, :], w2_rows[:, 0 : PACK - 1, :])
 
         pages = []
         relus = []
@@ -69,8 +70,7 @@ def tile_picked_dhlsendmxpagez_none_p_kernel(tc, x_words, x_scales, w1, w2, gn, 
         for i in range(2):
             nc.sync.dma_start(x_plane[2 + i : P : 32, :].bitcast(I32), picked_scales[16 + i : P : 32, :].bitcast(I32))
 
-        w2_last = keep.tile([P, H], F32, name="w2_last")
-        nc.sync.dma_start(w2_last[:], w2_rows[:, PACK - 1, :])
+        nc.sync.dma_start(raw["w2"][:, PACK - 1, :], w2_rows[:, PACK - 1, :])
         nc.sync.dma_start(lists["n1"][:], n1)
         gain = keep.tile([P, PACK], F32, name="gain")
         nc.sync.dma_start(gain[:], gn.rearrange("(p t) o -> p (t o)", t=PACK))
@@ -112,44 +112,44 @@ def tile_picked_dhlsendmxpagez_none_p_kernel(tc, x_words, x_scales, w1, w2, gn, 
             nc.vector.tensor_copy(words[:], word_table[:].indirect(lists[name][:]))
             picked.append(words)
 
-        w2_mx = []
-        w2_grouped = []
-        early = w2_early[:].rearrange("p j (m t) -> p m j t", t=PACK)
-        last = w2_last[:].rearrange("p (m t) -> p m t", t=PACK)
-        for half in range(2):
-            grouped = keep.tile([P, 2 * PACK * P], BF16, name="grouped_w2_%d" % half, align_bytes=64)
-            dealt = grouped[:].rearrange("p (t m j) -> p m j t", t=2, j=PACK)
-            cast(half, dealt[:, :, 0 : PACK - 1, :], early[:, :, :, 2 * half : 2 * half + 2])
-            w2_grouped.append(grouped)
-            w2_mx.append(mx_tiles("w2_%d" % half, 2 * P))
-        dealt = w2_grouped[0][:].rearrange("p (t m j) -> p m j t", t=2, j=PACK)
+        source = raw["w2"][:].rearrange("p j (m t) -> p m j t", t=PACK)
+        w2_mx = [mx_tiles("w2_%d" % half, 2 * P) for half in range(2)]
+        grouped = [keep.tile([P, 2 * PACK * P], BF16, name="grouped_w2_%d" % half, align_bytes=64) for half in range(2)]
+        dealt = [g[:].rearrange("p (t m j) -> p m j t", t=2, j=PACK) for g in grouped]
+        cast(0, dealt[0][:, :, 0:3, :], source[:, :, 0:3, 0:2])
+        cast(1, dealt[1][:, :, 0:2, :], source[:, :, 0:2, 2:4])
         for t in range(2):
-            cast(0, dealt[:, :, PACK - 1, t], last[:, :, t])
-            quantize(w2_mx[0], w2_grouped[0], t * P, P)
-        dealt = w2_grouped[1][:].rearrange("p (t m j) -> p m j t", t=2, j=PACK)
-        cast(1, dealt[:, :, PACK - 1, :], last[:, :, 2:4])
-        quantize(w2_mx[1], w2_grouped[1], 0, 2 * P)
+            cast(0, dealt[0][:, :, 3, t], source[:, :, 3, t])
+            quantize(w2_mx[0], grouped[0], t * P, P)
+        cast(0, dealt[1][:, :, 2:4, :], source[:, :, 2:4, 2:4])
+        quantize(w2_mx[1], grouped[1], 0, 2 * P)
 
+        halves = [slice(0, S // 2), slice(S // 2, S)]
         gained = []
         sent = []
         for t in range(PACK):
             cols = slice(t % 2 * P, (t % 2 + 1) * P)
-            y_bank = psum.tile([P, S], F32, name="y%d" % t)
-            for u, (codes, plane) in enumerate((w1_mx[t // 2], w2_mx[t // 2])):
-                nc.tensor.matmul_mx(
-                    out=y_bank[:],
-                    lhsT=codes[:, cols].bitcast(FP8X4),
-                    lhsT_scale=plane[:, cols],
-                    rhs=picked[u][:].bitcast(FP8X4),
-                    rhs_scale=x_plane[:, u * S : (u + 1) * S],
-                    start=(u == 0),
-                    stop=(u == 1),
-                )
             gy = keep.tile([P, S], F32, name="gy%d" % t)
-            nc.vector.tensor_scalar(gy[:], y_bank[:], gain[:, t : t + 1], None, ALU.mult)
-            gained.append(gy)
             ds = keep.tile([P, SEND_WINDOW], F32, name="ds%d" % t)
-            nc.scalar.activation(ds[:].indirect(lists["n1"][:]), gy[:], COPY)
+            for v, places in enumerate(halves if t == 0 else [slice(0, S)]):
+                y_bank = psum.tile([P, places.stop - places.start], F32, name="y%d_%d" % (t, v), tag="bank%d" % (t + v * PACK))
+                for u, (codes, plane) in enumerate((w1_mx[t // 2], w2_mx[t // 2])):
+                    nc.tensor.matmul_mx(
+                        out=y_bank[:],
+                        lhsT=codes[:, cols].bitcast(FP8X4),
+                        lhsT_scale=plane[:, cols],
+                        rhs=picked[u][:, places].bitcast(FP8X4),
+                        rhs_scale=x_plane[:, u * S + places.start : u * S + places.stop],
+                        start=(u == 0),
+                        stop=(u == 1),
+                    )
+                if t == 0 and v == 0:
+                    nc.scalar.activation(gy[:, places], y_bank[:], COPY, scale=gain[:, t : t + 1])
+                else:
+                    nc.vector.tensor_scalar(gy[:, places], y_bank[:], gain[:, t : t + 1], None, ALU.mult)
+                entries = lists["n1"][:, places.start // 16 : places.stop // 16]
+                nc.scalar.activation(ds[:].indirect(entries), gy[:, places], COPY)
+            gained.append(gy)
             sent.append(ds)
 
         grouped = keep.tile([P, PACK * N], BF16, name="grouped_w3", tag="grouped_w3", align_bytes=64)
@@ -164,7 +164,6 @@ def tile_picked_dhlsendmxpagez_none_p_kernel(tc, x_words, x_scales, w1, w2, gn, 
         z_slots = z[:].rearrange("p (c t) -> p t c", t=PACK)
         for t in range(PACK - 1):
             nc.vector.tensor_tensor(z_slots[:, t, :], gained[t][:], sent[t][:, 0:S], ALU.subtract)
-        halves = [slice(0, S // 2), slice(S // 2, S)]
         for places in halves:
             nc.vector.tensor_tensor(z_slots[:, PACK - 1, places], gained[-1][:, places], sent[-1][:, places], ALU.subtract)
         z_mx = mx_tiles("z", S)
@@ -173,10 +172,12 @@ def tile_picked_dhlsendmxpagez_none_p_kernel(tc, x_words, x_scales, w1, w2, gn, 
 
         for m in range(N // P):
             cols = slice(m * P, (m + 1) * P)
-            h_bank = psum.tile([P, S], F32, name="h%d" % m)
-            for places in halves if m == 0 else [slice(0, S)]:
+            pieces = halves if m == 0 else [slice(0, S)]
+            banks = []
+            for u, places in enumerate(pieces):
+                h_bank = psum.tile([P, places.stop - places.start], F32, name="h%d_%d" % (m, u), tag="bank%d" % (PACK + 1 + m if u == 0 and m < 3 else u))
                 nc.tensor.matmul_mx(
-                    out=h_bank[:, places],
+                    out=h_bank[:],
                     lhsT=w3_mx[0][:, cols].bitcast(FP8X4),
                     lhsT_scale=w3_mx[1][:, cols],
                     rhs=z_mx[0][:, places].bitcast(FP8X4),
@@ -184,10 +185,15 @@ def tile_picked_dhlsendmxpagez_none_p_kernel(tc, x_words, x_scales, w1, w2, gn, 
                     start=True,
                     stop=True,
                 )
-            nc.vector.tensor_scalar(relus[m][:, 0:S], h_bank[:], 0.0, None, ALU.max)
+                banks.append(h_bank)
+                if u == 1:
+                    nc.scalar.activation(relus[m][:, places], h_bank[:], RELU)
+                else:
+                    nc.vector.tensor_scalar(relus[m][:, places], h_bank[:], 0.0, None, ALU.max)
             fetched = keep.tile([P, S], F32, name="fetched%d" % m)
             nc.scalar.activation(fetched[:], relus[m][:].indirect(lists["n3"][:]), COPY)
             nw = keep.tile([P, S], F32, name="nw%d" % m)
-            nc.vector.tensor_tensor(nw[:], h_bank[:], fetched[:], ALU.subtract)
+            for places, h_bank in zip(pieces, banks):
+                nc.vector.tensor_tensor(nw[:, places], h_bank[:], fetched[:, places], ALU.subtract)
             nc.scalar.activation(pages[m][:].indirect(lists["n2"][:]), nw[:], COPY)
             nc.sync.dma_start(out[cols, :], pages[m][:])

from contextlib import ExitStack

import concourse.mybir as mybir

K, T, S, N, H, U = 512, 2048, 256, 512, 512, 1024
FLOPS = 2 * (2 * K * H * S + H * N * S)

F32 = mybir.dt.float32
BF16 = mybir.dt.bfloat16
I32 = mybir.dt.int32
U32 = mybir.dt.uint32
U16 = mybir.dt.uint16
U8 = mybir.dt.uint8
FP8X4 = mybir.dt.float8_e4m3fn_x4
ALU = mybir.AluOpType
COPY = mybir.ActivationFunctionType.Copy
RELU = mybir.ActivationFunctionType.Relu

P = 128
PACK = 4
SEND_WINDOW = 2 * S
FETCH_WINDOW = S + 16


def tile_picked_dhlsendmxpagez_none_p_kernel(tc, x_words, x_scales, w1, w2, gn, w3, offs, hz, n1, n2, n3, out):
    nc = tc.nc
    with ExitStack() as ctx:
        keep = ctx.enter_context(tc.tile_pool(name="keep", bufs=1))
        psum = ctx.enter_context(tc.psum_pool(name="psum", bufs=1))

        lists = {}
        for name in ("offs", "hz", "n1", "n3", "n2"):
            lists[name] = keep.tile([P, S // 16], U16, name="list_" + name)
        raw = {}
        w1_rows = w1.rearrange("(p j) c -> p j c", j=PACK)
        raw["w1"] = keep.tile([P, PACK, H], F32, name="raw_w1")
        nc.sync.dma_start(raw["w1"][:, 0:2, :], w1_rows[:, 0:2, :])
        nc.sync.dma_start(lists["offs"][:], offs)
        nc.sync.dma_start(lists["hz"][:], hz)

        scale_table = keep.tile([P, T], U8, name="scale_table")
        nc.vector.memset(scale_table[:].bitcast(I32), 0)
        for i in range(2):
            nc.sync.dma_start(scale_table[i:P:16, :].bitcast(I32), x_scales[0, i:16:2, :].bitcast(I32))

        nc.sync.dma_start(raw["w1"][:, 2:4, :], w1_rows[:, 2:4, :])
        word_table = keep.tile([P, T], U32, name="word_table")
        nc.sync.dma_start(word_table[:].bitcast(I32), x_words[0].rearrange("p c r -> p (c r)").bitcast(I32))
        w2_rows = w2.rearrange("(p j) c -> p j c", j=PACK)
        raw["w2"] = keep.tile([P, PACK, H], F32, name="raw_w2")
        nc.sync.dma_start(raw["w2"][:, 0 : PACK - 1, :], w2_rows[:, 0 : PACK - 1, :])

        pages = []
        relus = []
        for m in range(N // P):
            page = keep.tile([P, U], F32, name="page%d" % m)
            if m < 2:
                nc.vector.memset(page[:].bitcast(I32), 0)
            else:
                nc.scalar.activation(page[:], pages[m - 2][:], COPY)
            pages.append(page)
            relu_h = keep.tile([P, FETCH_WINDOW], F32, name="relu%d" % m)
            relus.append(relu_h)

        picked_scales = keep.tile([P, 2 * S], U8, name="picked_scales")
        for u, name in enumerate(("offs", "hz")):
            nc.vector.tensor_copy(picked_scales[:, u * S : (u + 1) * S], scale_table[:].indirect(lists[name][:]))
        x_plane = keep.tile([P, 2 * S], U8, name="x_plane", align_bytes=64)
        nc.vector.tensor_copy(x_plane[:].bitcast(I32), picked_scales[:].bitcast(I32))
        for i in range(2):
            nc.sync.dma_start(x_plane[2 + i : P : 32, :].bitcast(I32), picked_scales[16 + i : P : 32, :].bitcast(I32))

        nc.sync.dma_start(raw["w2"][:, PACK - 1, :], w2_rows[:, PACK - 1, :])
        nc.sync.dma_start(lists["n1"][:], n1)
        gain = keep.tile([P, PACK], F32, name="gain")
        nc.sync.dma_start(gain[:], gn.rearrange("(p t) o -> p (t o)", t=PACK))
        raw["w3"] = keep.tile([P, PACK, N], F32, name="raw_w3")
        nc.sync.dma_start(raw["w3"][:], w3.rearrange("(p j) c -> p j c", j=PACK))
        nc.sync.dma_start(lists["n3"][:], n3)
        nc.sync.dma_start(lists["n2"][:], n2)

        def mx_tiles(name, width):
            codes = keep.tile([P, width], U32, name="codes_" + name, align_bytes=64)
            plane = keep.tile([P, width], U8, name="plane_" + name, align_bytes=64)
            return codes, plane

        def quantize(operand, grouped, first, width):
            codes, plane = operand
            nc.vector.quantize_mx(
                out=codes[:, first : first + width].bitcast(FP8X4),
                scales=plane[:, first : first + width],
                in_=grouped[:, PACK * first : PACK * (first + width)],
            )

        def cast(half, dealt, source):
            if half == 0:
                nc.vector.tensor_copy(dealt, source)
            else:
                nc.scalar.activation(dealt, source, COPY)

        w1_mx = []
        for half in range(2):
            grouped = keep.tile([P, 2 * PACK * P], BF16, name="grouped_w1_%d" % half, align_bytes=64)
            dealt = grouped[:].rearrange("p (t m j) -> p m j t", t=2, j=PACK)
            cast(half, dealt, raw["w1"][:].rearrange("p j (m t) -> p m j t", t=PACK)[:, :, :, 2 * half : 2 * half + 2])
            w1_mx.append(mx_tiles("w1_%d" % half, 2 * P))
            quantize(w1_mx[half], grouped, 0, 2 * P)

        picked = []
        for name in ("offs", "hz"):
            words = keep.tile([P, S], U32, name="picked_" + name, align_bytes=64)
            nc.vector.tensor_copy(words[:], word_table[:].indirect(lists[name][:]))
            picked.append(words)

        source = raw["w2"][:].rearrange("p j (m t) -> p m j t", t=PACK)
        w2_mx = [mx_tiles("w2_%d" % half, 2 * P) for half in range(2)]
        grouped = [keep.tile([P, 2 * PACK * P], BF16, name="grouped_w2_%d" % half, align_bytes=64) for half in range(2)]
        dealt = [g[:].rearrange("p (t m j) -> p m j t", t=2, j=PACK) for g in grouped]
        cast(0, dealt[0][:, :, 0:3, :], source[:, :, 0:3, 0:2])
        cast(1, dealt[1][:, :, 0:2, :], source[:, :, 0:2, 2:4])
        for t in range(2):
            cast(0, dealt[0][:, :, 3, t], source[:, :, 3, t])
            quantize(w2_mx[0], grouped[0], t * P, P)
        cast(0, dealt[1][:, :, 2:4, :], source[:, :, 2:4, 2:4])
        quantize(w2_mx[1], grouped[1], 0, 2 * P)

        halves = [slice(0, S // 2), slice(S // 2, S)]
        gained = []
        sent = []
        for t in range(PACK):
            cols = slice(t % 2 * P, (t % 2 + 1) * P)
            gy = keep.tile([P, S], F32, name="gy%d" % t)
            ds = keep.tile([P, SEND_WINDOW], F32, name="ds%d" % t)
            for v, places in enumerate(halves if t == 0 else [slice(0, S)]):
                y_bank = psum.tile([P, places.stop - places.start], F32, name="y%d_%d" % (t, v), tag="bank%d" % (t + v * PACK))
                for u, (codes, plane) in enumerate((w1_mx[t // 2], w2_mx[t // 2])):
                    nc.tensor.matmul_mx(
                        out=y_bank[:],
                        lhsT=codes[:, cols].bitcast(FP8X4),
                        lhsT_scale=plane[:, cols],
                        rhs=picked[u][:, places].bitcast(FP8X4),
                        rhs_scale=x_plane[:, u * S + places.start : u * S + places.stop],
                        start=(u == 0),
                        stop=(u == 1),
                    )
                if t == 0 and v == 0:
                    nc.scalar.activation(gy[:, places], y_bank[:], COPY, scale=gain[:, t : t + 1])
                else:
                    nc.vector.tensor_scalar(gy[:, places], y_bank[:], gain[:, t : t + 1], None, ALU.mult)
                entries = lists["n1"][:, places.start // 16 : places.stop // 16]
                nc.scalar.activation(ds[:].indirect(entries), gy[:, places], COPY)
            gained.append(gy)
            sent.append(ds)

        grouped = keep.tile([P, PACK * N], BF16, name="grouped_w3", tag="grouped_w3", align_bytes=64)
        nc.vector.tensor_copy(
            grouped[:].rearrange("p (c i j) -> p c j i", i=4, j=PACK),
            raw["w3"][:].rearrange("p j (c i) -> p c j i", i=4),
        )
        w3_mx = mx_tiles("w3", N)
        quantize(w3_mx, grouped, 0, N)

        z = keep.tile([P, S * PACK], BF16, name="z", tag="grouped_w3", align_bytes=64)
        z_slots = z[:].rearrange("p (c t) -> p t c", t=PACK)
        for t in range(PACK - 1):
            nc.vector.tensor_tensor(z_slots[:, t, :], gained[t][:], sent[t][:, 0:S], ALU.subtract)
        for places in halves:
            nc.vector.tensor_tensor(z_slots[:, PACK - 1, places], gained[-1][:, places], sent[-1][:, places], ALU.subtract)
        z_mx = mx_tiles("z", S)
        for places in halves:
            quantize(z_mx, z, places.start, S // 2)

        for m in range(N // P):
            cols = slice(m * P, (m + 1) * P)
            pieces = halves if m == 0 else [slice(0, S)]
            banks = []
            for u, places in enumerate(pieces):
                h_bank = psum.tile([P, places.stop - places.start], F32, name="h%d_%d" % (m, u), tag="bank%d" % (PACK + 1 + m if u == 0 and m < 3 else u))
                nc.tensor.matmul_mx(
                    out=h_bank[:],
                    lhsT=w3_mx[0][:, cols].bitcast(FP8X4),
                    lhsT_scale=w3_mx[1][:, cols],
                    rhs=z_mx[0][:, places].bitcast(FP8X4),
                    rhs_scale=z_mx[1][:, places],
                    start=True,
                    stop=True,
                )
                banks.append(h_bank)
                if u == 1:
                    nc.scalar.activation(relus[m][:, places], h_bank[:], RELU)
                else:
                    nc.vector.tensor_scalar(relus[m][:, places], h_bank[:], 0.0, None, ALU.max)
            fetched = keep.tile([P, S], F32, name="fetched%d" % m)
            nc.scalar.activation(fetched[:], relus[m][:].indirect(lists["n3"][:]), COPY)
            nw = keep.tile([P, S], F32, name="nw%d" % m)
            for places, h_bank in zip(pieces, banks):
                nc.vector.tensor_tensor(nw[:, places], h_bank[:], fetched[:, places], ALU.subtract)
            nc.scalar.activation(pages[m][:].indirect(lists["n2"][:]), nw[:], COPY)
            nc.sync.dma_start(out[cols, :], pages[m][:])
